import numpy as np
import ml_dtypes


def mxq(x, axis, fmt="e4m3"):
    dtype, down = {"e4m3": (ml_dtypes.float8_e4m3fn, 7), "e5m2": (ml_dtypes.float8_e5m2, 14)}[fmt]
    v = np.moveaxis(np.asarray(x, np.float32).astype(ml_dtypes.bfloat16).astype(np.float64), axis, -1)
    blocks = v.reshape(v.shape[:-1] + (-1, 32))
    amax = np.abs(blocks).max(-1, keepdims=True)
    byte = np.maximum(np.where(amax > 0, np.frexp(amax)[1] - 1 + 127, 0) - down, 1)
    scale = np.exp2(byte - 127.0)
    codes = (blocks / scale).astype(np.float32).astype(dtype).astype(np.float64)
    return np.moveaxis((codes * scale).reshape(v.shape), -1, axis)


WIDE = False


def mx_kscale(k):
    if not WIDE:
        return np.ones(k)
    levels = np.array([10, -10, 5, -5, 0])
    if k % 512:
        return np.exp2(np.random.permutation(np.resize(levels, k // 32))).repeat(32)
    a = np.empty((k // 512, 16))
    for p in range(k // 512):
        a[p, :8] = np.random.permutation(np.resize(levels, 8))
        for g in range(8):
            far = levels[np.abs(levels - a[p, g]) >= 10]
            a[p, g + 8] = far[np.random.randint(len(far))]
    return np.exp2(a.ravel()).repeat(32)


def f64(x):
    return np.asarray(x).astype(np.float64)


def striped(idx):
    return np.tile(idx.reshape(-1, 16).T, (8, 1)).astype(np.uint16)


def unstriped(offs):
    return offs[:16].T.reshape(-1).astype(np.int64)


def relu2(v):
    return np.maximum(v, 0.0) ** 2


K, T, E, C, N = 512, 1536, 12, 128, 256
M = 1024


def by_expert(wq, xq):
    return np.concatenate([wq[e].T @ xq[:, e * C:(e + 1) * C] for e in range(E)], axis=1)


def setup_inputs():
    n = np.random.standard_normal
    s = mx_kscale(K)[:, None]
    r = mx_kscale(M)[:, None]
    return {
        "uT": (n((M, T)) * r).astype(np.float32),
        "wu": (n((M, K)) / np.sqrt(M) / r * s.T).astype(np.float32),
        "w": (n((E, K, N)) / np.sqrt(K) / s[None]).astype(np.float32),
        "b": (0.3 * n((N, E))).astype(np.float32),
        "gate": np.tile(np.random.uniform(0.2, 1.0, E * C), (N, 1)).astype(np.float32),
        "offs": striped(np.random.permutation(T)[:E * C]),
    }


def reference(uT, wu, w, b, gate, offs):
    idx = unstriped(offs)
    x = mxq(f64(wu), 0, "e4m3").T @ mxq(f64(uT), 0, "e4m3")
    xq = mxq(x[:, idx], 0, "e4m3")
    y = by_expert(mxq(f64(w), 1, "e4m3"), xq)
    y = relu2(y + np.repeat(f64(b), C, axis=1))
    out = np.zeros((N, T))
    out[:, idx] = f64(gate) * y
    return out

@@ -1,0 +1,231 @@
+from contextlib import ExitStack
+
+import concourse.mybir as mybir
+
+K, T, E, C, N, M = 512, 1536, 12, 128, 256, 1024
+FLOPS = 2 * M * K * T + 2 * K * N * E * C
+
+F32 = mybir.dt.float32
+BF16 = mybir.dt.bfloat16
+U32 = mybir.dt.uint32
+U16 = mybir.dt.uint16
+U8 = mybir.dt.uint8
+FP8X4 = mybir.dt.float8_e4m3fn_x4
+ACT = mybir.ActivationFunctionType
+MULT = mybir.AluOpType.mult
+
+P = 128
+PACK = 4
+K_PASS = P * PACK
+PASSES = M // K_PASS
+SUB = 256
+TOKEN_LOADS = ((0, 512), (512, 512), (1024, 256), (1280, 256))
+SCALAR_CASTS = {(1, 0), (0, 512), (0, 1024)}
+GATHERS = ((0, 256), (256, 256), (512, 512), (1024, 512))
+GATE_LOAD = 512
+PAIR = 2 * C
+
+
+def tile_moe_prv_lin_relu2_kernel(tc, uT, wu, w, b, gate, offs, out):
+    nc = tc.nc
+
+    with ExitStack() as ctx:
+        keep = ctx.enter_context(tc.tile_pool(name="keep", bufs=1))
+        raws = ctx.enter_context(tc.tile_pool(name="raws", bufs=11))
+        ring = ctx.enter_context(tc.tile_pool(name="ring", bufs=3))
+        psum = ctx.enter_context(tc.psum_pool(name="psum", bufs=8))
+
+        offsets = keep.tile([P, T // 16], U16, name="offsets")
+
+        def load(rows, shape):
+            raw = raws.tile(shape, F32, name="raw", tag="raw")
+            nc.sync.dma_start(out=raw[:], in_=rows)
+            return raw
+
+        def mx_tiles(name, width):
+            codes = keep.tile([P, width], U32, name=name + "_codes", align_bytes=64)
+            scales = keep.tile([P, width], U8, name=name + "_scales", align_bytes=64)
+            return codes, scales
+
+        def quantize(mx, cols, grouped):
+            nc.vector.quantize_mx(out=mx[0][:, cols].bitcast(FP8X4), scales=mx[1][:, cols], in_=grouped)
+
+        def interleave(copy, grouped, rows):
+            copy(
+                out=grouped.rearrange("p (c i j) -> p c j i", i=4, j=PACK),
+                in_=rows.rearrange("p j (c i) -> p c j i", i=4),
+            )
+
+        def matmul(acc, lhs, lhs_cols, rhs, rhs_cols, start, stop):
+            nc.tensor.matmul_mx(
+                out=acc,
+                lhsT=lhs[0][:, lhs_cols].bitcast(FP8X4),
+                lhsT_scale=lhs[1][:, lhs_cols],
+                rhs=rhs[0][:, rhs_cols].bitcast(FP8X4),
+                rhs_scale=rhs[1][:, rhs_cols],
+                start=start,
+                stop=stop,
+            )
+
+        wu_raw, u_raw = {}, {}
+
+        def load_wu(g):
+            rows = wu[g * K_PASS : (g + 1) * K_PASS, :].rearrange("(p j) c -> p j c", j=PACK)
+            wu_raw[g] = load(rows, [P, PACK, K])
+
+        def load_u(g, t0, width):
+            rows = uT[g * K_PASS : (g + 1) * K_PASS, t0 : t0 + width].rearrange("(p j) t -> p j t", j=PACK)
+            u_raw[g, t0] = load(rows, [P, PACK, width])
+
+        for t0, width in TOKEN_LOADS:
+            for g in range(PASSES):
+                if t0 == 0:
+                    load_wu(g)
+                load_u(g, t0, width)
+        nc.sync.dma_start(offsets[:], offs)
+        bias = keep.tile([P, 2, E], F32, name="bias")
+        nc.sync.dma_start(out=bias[:], in_=b.rearrange("(h p) e -> p h e", p=P))
+        gates = keep.tile([P, 2, T], F32, name="gates")
+        w_raw = []
+        for q in range(E // 2):
+            rows = w[2 * q : 2 * q + 2].rearrange("e (p j) n -> p e (j n)", j=PACK)
+            w_raw.append(load(rows, [P, 2, PACK * N]))
+            if 2 <= q < 2 + T // GATE_LOAD:
+                cols = slice((q - 2) * GATE_LOAD, (q - 1) * GATE_LOAD)
+                nc.sync.dma_start(out=gates[:, :, cols], in_=gate[:, cols].rearrange("(h p) s -> p h s", p=P))
+
+        wu_mx = [mx_tiles("wu%d" % g, K) for g in range(PASSES)]
+        u_mx = [mx_tiles("u%d" % g, T) for g in range(PASSES)]
+        x_pairs = [keep.tile([P, 2 * T], BF16, name="x_pairs%d" % a) for a in range(2)]
+
+        def prepare_wu(g):
+            grouped = ring.tile([P, K * PACK], BF16, name="wu_grouped", tag="w_grouped", align_bytes=64)
+            copy = nc.scalar.copy if g == 0 else nc.vector.tensor_copy
+            copy(
+                out=grouped[:].rearrange("p (t m j) -> p m t j", t=PACK, j=PACK),
+                in_=wu_raw[g][:].rearrange("p j (m t) -> p m t j", t=PACK),
+            )
+            quantize(wu_mx[g], slice(0, K), grouped[:])
+
+        def prepare_u(g, t0, width):
+            raw = u_raw[g, t0]
+            if (g, t0) in SCALAR_CASTS:
+                parts = [(nc.scalar.copy, 0, SUB)] + [(nc.vector.tensor_copy, s, SUB) for s in range(SUB, width, SUB)]
+            else:
+                parts = [(nc.vector.tensor_copy, 0, width)]
+            made = []
+            for copy, s, n in parts:
+                grouped = ring.tile([P, n * PACK], BF16, name="u_grouped", tag="u_grouped", bufs=4, align_bytes=64)
+                interleave(copy, grouped[:], raw[:, :, s : s + n])
+                made.append((grouped, slice(t0 + s, t0 + s + n)))
+            for grouped, cols in reversed(made):
+                quantize(u_mx[g], cols, grouped[:])
+
+        def project(t0):
+            cols = slice(t0, t0 + SUB)
+            last = t0 + SUB == T
+            for a in range(2):
+                acc = psum.tile([P, 2, SUB], F32, name="acc", tag="acc")
+                for e in range(2):
+                    j = 2 * a + e
+                    for g in range(PASSES):
+                        matmul(acc[:, e, :], wu_mx[g], slice(j * P, (j + 1) * P), u_mx[g], cols, g == 0, g == PASSES - 1)
+                copy = nc.vector.tensor_copy if (last and a == 1) else nc.scalar.copy
+                copy(
+                    out=x_pairs[a][:, 2 * t0 : 2 * (t0 + SUB)].rearrange("p (n e) -> p n e", e=2),
+                    in_=acc[:].rearrange("p e n -> p n e"),
+                )
+
+        prepare_wu(0)
+        prepare_u(0, *TOKEN_LOADS[0])
+        prepare_wu(1)
+        for i, (t0, width) in enumerate(TOKEN_LOADS):
+            prepare_u(1, t0, width)
+            if i + 1 < len(TOKEN_LOADS):
+                prepare_u(0, *TOKEN_LOADS[i + 1])
+            for s in reversed(range(t0, t0 + width, SUB)):
+                project(s)
+
+        x_mx = mx_tiles("x", T)
+        w_mx = mx_tiles("w", E * N)
+        windows = [keep.tile([P, T], F32, name="window%d" % h) for h in range(2)]
+        picked = {}
+
+        def slot_offsets(s0, n):
+            return offsets[:, s0 // 16 : (s0 + n) // 16]
+
+        def gather(i):
+            s0, n = GATHERS[i]
+            tag = "slots%d" % (i - 2) if i >= 2 else "picked%d" % i
+            picked[i] = keep.tile([P, 2, 2 * n], BF16, name="picked", tag=tag, align_bytes=64)
+            for a in range(2):
+                nc.vector.tensor_copy(
+                    out=picked[i][:, a, :].bitcast(U32),
+                    in_=x_pairs[a][:].bitcast(U32).indirect(slot_offsets(s0, n)),
+                )
+
+        def prepare_x(i):
+            s0, n = GATHERS[i]
+            grouped = keep.tile([P, n * PACK], BF16, name="x_grouped", tag="slots%d" % i, align_bytes=64)
+            nc.scalar.copy(
+                out=grouped[:].bitcast(F32).rearrange("p (s a) -> p s a", a=2),
+                in_=picked[i][:].bitcast(F32).rearrange("p a s -> p s a"),
+            )
+            quantize(x_mx, slice(s0, s0 + n), grouped[:])
+
+        def prepare_w(q):
+            grouped = ring.tile([P, 2 * N * PACK], BF16, name="w_grouped", tag="w_grouped", align_bytes=64)
+            for e in range(2):
+                interleave(
+                    nc.scalar.copy,
+                    grouped[:, e * N * PACK : (e + 1) * N * PACK],
+                    w_raw[q][:, e, :].rearrange("p (j n) -> p j n", j=PACK),
+                )
+            quantize(w_mx, slice(2 * q * N, 2 * (q + 1) * N), grouped[:])
+
+        def experts(e0, count, h):
+            width = count * C
+            acc = psum.tile([P, width], F32, name="acc", tag="acc")
+            relu = ring.tile([P, width], F32, name="relu", tag="relu%d" % count, bufs=3 if count == 2 else 1)
+            for i in range(count):
+                e = e0 + i
+                matmul(acc[:, i * C : (i + 1) * C], w_mx, slice(e * N + h * P, e * N + (h + 1) * P),
+                       x_mx, slice(e * C, (e + 1) * C), True, True)
+            for i in range(count):
+                nc.scalar.activation(out=relu[:, i * C : (i + 1) * C], in_=acc[:, i * C : (i + 1) * C],
+                                     func=ACT.Relu, bias=bias[:, h, e0 + i : e0 + i + 1])
+            squared = ring.tile([P, width], F32, name="squared", tag="squared", bufs=6)
+            nc.scalar.activation(out=squared[:], in_=relu[:], func=ACT.Square)
+            nc.vector.tensor_tensor(
+                windows[h][:].indirect(slot_offsets(e0 * C, width)),
+                squared[:],
+                gates[:, h, e0 * C : e0 * C + width],
+                MULT,
+            )
+            if e0 + count == E:
+                nc.sync.dma_start(out=out[h * P : (h + 1) * P, :], in_=windows[h][:])
+
+        gather(0)
+        gather(1)
+        prepare_w(0)
+        prepare_x(0)
+        gather(2)
+        prepare_x(1)
+        prepare_w(1)
+        gather(3)
+        experts(0, 2, 0)
+        prepare_x(2)
+        experts(0, 2, 1)
+        prepare_w(2)
+        prepare_x(3)
+        experts(2, 2, 0)
+        prepare_w(3)
+        experts(2, 2, 1)
+        experts(4, 2, 0)
+        prepare_w(4)
+        experts(4, 2, 1)
+        prepare_w(5)
+        experts(6, 2, 0)
+        experts(6, 2, 1)
+        experts(8, 4, 0)
+        experts(8, 4, 1)

@@ -20,8 +20,7 @@ K_PASS = P * PACK
 PASSES = M // K_PASS
 SUB = 256
 TOKEN_LOADS = ((0, 512), (512, 512), (1024, 256), (1280, 256))
-SCALAR_CASTS = {(1, 0), (0, 512), (0, 1024)}
-GATHERS = ((0, 256), (256, 256), (512, 512), (1024, 512))
+GATHERS = ((0, 512), (512, 512), (1024, 512))
 GATE_LOAD = 512
 PAIR = 2 * C
 
@@ -98,53 +97,61 @@ def tile_moe_prv_lin_relu2_kernel(tc, uT, wu, w, b, gate, offs, out):
         u_mx = [mx_tiles("u%d" % g, T) for g in range(PASSES)]
         x_pairs = [keep.tile([P, 2 * T], BF16, name="x_pairs%d" % a) for a in range(2)]
 
-        def prepare_wu(g):
+        def cast_wu(copy, g):
             grouped = ring.tile([P, K * PACK], BF16, name="wu_grouped", tag="w_grouped", align_bytes=64)
-            copy = nc.scalar.copy if g == 0 else nc.vector.tensor_copy
             copy(
                 out=grouped[:].rearrange("p (t m j) -> p m t j", t=PACK, j=PACK),
                 in_=wu_raw[g][:].rearrange("p j (m t) -> p m t j", t=PACK),
             )
-            quantize(wu_mx[g], slice(0, K), grouped[:])
+            return wu_mx[g], slice(0, K), grouped[:]
 
-        def prepare_u(g, t0, width):
-            raw = u_raw[g, t0]
-            if (g, t0) in SCALAR_CASTS:
-                parts = [(nc.scalar.copy, 0, SUB)] + [(nc.vector.tensor_copy, s, SUB) for s in range(SUB, width, SUB)]
-            else:
-                parts = [(nc.vector.tensor_copy, 0, width)]
-            made = []
-            for copy, s, n in parts:
-                grouped = ring.tile([P, n * PACK], BF16, name="u_grouped", tag="u_grouped", bufs=4, align_bytes=64)
-                interleave(copy, grouped[:], raw[:, :, s : s + n])
-                made.append((grouped, slice(t0 + s, t0 + s + n)))
-            for grouped, cols in reversed(made):
-                quantize(u_mx[g], cols, grouped[:])
+        def cast_u(copy, g, t0, n):
+            start = max(s for s, width in TOKEN_LOADS if s <= t0)
+            grouped = ring.tile([P, n * PACK], BF16, name="u_grouped", tag="u_grouped", bufs=4, align_bytes=64)
+            interleave(copy, grouped[:], u_raw[g, start][:, :, t0 - start : t0 - start + n])
+            return u_mx[g], slice(t0, t0 + n), grouped[:]
 
-        def project(t0):
-            cols = slice(t0, t0 + SUB)
-            last = t0 + SUB == T
+        def project(t0, n, copies):
+            cols = slice(t0, t0 + n)
             for a in range(2):
-                acc = psum.tile([P, 2, SUB], F32, name="acc", tag="acc")
+                acc = psum.tile([P, 2, n], F32, name="acc", tag="acc")
                 for e in range(2):
                     j = 2 * a + e
                     for g in range(PASSES):
                         matmul(acc[:, e, :], wu_mx[g], slice(j * P, (j + 1) * P), u_mx[g], cols, g == 0, g == PASSES - 1)
-                copy = nc.vector.tensor_copy if (last and a == 1) else nc.scalar.copy
-                copy(
-                    out=x_pairs[a][:, 2 * t0 : 2 * (t0 + SUB)].rearrange("p (n e) -> p n e", e=2),
+                copies[a](
+                    out=x_pairs[a][:, 2 * t0 : 2 * (t0 + n)].rearrange("p (n e) -> p n e", e=2),
                     in_=acc[:].rearrange("p e n -> p n e"),
                 )
 
-        prepare_wu(0)
-        prepare_u(0, *TOKEN_LOADS[0])
-        prepare_wu(1)
-        for i, (t0, width) in enumerate(TOKEN_LOADS):
-            prepare_u(1, t0, width)
-            if i + 1 < len(TOKEN_LOADS):
-                prepare_u(0, *TOKEN_LOADS[i + 1])
-            for s in reversed(range(t0, t0 + width, SUB)):
-                project(s)
+        on_s, on_v = nc.scalar.copy, nc.vector.tensor_copy
+        wu0 = cast_wu(on_s, 0)
+        u00 = cast_u(on_v, 0, 0, 512)
+        quantize(*wu0)
+        quantize(*u00)
+        quantize(*cast_wu(on_v, 1))
+        u10a = cast_u(on_s, 1, 0, 256)
+        quantize(*cast_u(on_v, 1, 256, 256))
+        quantize(*u10a)
+        project(256, 256, (on_s, on_s))
+        project(0, 256, (on_s, on_s))
+        quantize(*cast_u(on_v, 0, 512, 512))
+        quantize(*cast_u(on_v, 1, 512, 512))
+        u02 = cast_u(on_s, 0, 1024, 256)
+        project(512, 256, (on_s, on_s))
+        project(768, 256, (on_s, on_s))
+        u12 = cast_u(on_v, 1, 1024, 256)
+        quantize(*u02)
+        u03 = cast_u(on_v, 0, 1280, 256)
+        quantize(*u12)
+        project(1024, 256, (on_s, on_s))
+        u13a = cast_u(on_v, 1, 1280, 128)
+        quantize(*u03)
+        u13b = cast_u(on_v, 1, 1408, 128)
+        quantize(*u13a)
+        quantize(*u13b)
+        project(1280, 128, (on_s, on_s))
+        project(1408, 128, (on_v, on_s))
 
         x_mx = mx_tiles("x", T)
         w_mx = mx_tiles("w", E * N)
@@ -175,12 +182,10 @@ def tile_moe_prv_lin_relu2_kernel(tc, uT, wu, w, b, gate, offs, out):
 
         def prepare_w(q):
             grouped = ring.tile([P, 2 * N * PACK], BF16, name="w_grouped", tag="w_grouped", align_bytes=64)
-            for e in range(2):
-                interleave(
-                    nc.scalar.copy,
-                    grouped[:, e * N * PACK : (e + 1) * N * PACK],
-                    w_raw[q][:, e, :].rearrange("p (j n) -> p j n", j=PACK),
-                )
+            nc.scalar.copy(
+                out=grouped[:].rearrange("p (e c i j) -> p e c j i", e=2, i=4, j=PACK),
+                in_=w_raw[q][:].rearrange("p e (j c i) -> p e c j i", j=PACK, i=4),
+            )
             quantize(w_mx, slice(2 * q * N, 2 * (q + 1) * N), grouped[:])
 
         def experts(e0, count, h):
@@ -210,22 +215,20 @@ def tile_moe_prv_lin_relu2_kernel(tc, uT, wu, w, b, gate, offs, out):
         prepare_w(0)
         prepare_x(0)
         gather(2)
-        prepare_x(1)
         prepare_w(1)
-        gather(3)
+        prepare_x(1)
         experts(0, 2, 0)
-        prepare_x(2)
         experts(0, 2, 1)
-        prepare_w(2)
-        prepare_x(3)
+        prepare_x(2)
         experts(2, 2, 0)
-        prepare_w(3)
+        prepare_w(2)
         experts(2, 2, 1)
         experts(4, 2, 0)
-        prepare_w(4)
+        prepare_w(3)
         experts(4, 2, 1)
-        prepare_w(5)
         experts(6, 2, 0)
+        prepare_w(4)
+        prepare_w(5)
         experts(6, 2, 1)
         experts(8, 4, 0)
         experts(8, 4, 1)

@@ -13,6 +13,7 @@ U8 = mybir.dt.uint8
 FP8X4 = mybir.dt.float8_e4m3fn_x4
 ACT = mybir.ActivationFunctionType
 MULT = mybir.AluOpType.mult
+ADD = mybir.AluOpType.add
 
 P = 128
 PACK = 4
@@ -23,6 +24,8 @@ TOKEN_LOADS = ((0, 512), (512, 512), (1024, 256), (1280, 256))
 GATHERS = ((0, 512), (512, 512), (1024, 512))
 GATE_LOAD = 512
 PAIR = 2 * C
+RELU_SLOTS = (2, 1, 3, 4, 5, 0)
+W_SLOTS = ("w0", "wu0", "u0_0", "wu1", "u1_0", "u0_512")
 
 
 def tile_moe_prv_lin_relu2_kernel(tc, uT, wu, w, b, gate, offs, out):
@@ -30,14 +33,14 @@ def tile_moe_prv_lin_relu2_kernel(tc, uT, wu, w, b, gate, offs, out):
 
     with ExitStack() as ctx:
         keep = ctx.enter_context(tc.tile_pool(name="keep", bufs=1))
-        raws = ctx.enter_context(tc.tile_pool(name="raws", bufs=11))
+        raws = ctx.enter_context(tc.tile_pool(name="raws", bufs=1))
         ring = ctx.enter_context(tc.tile_pool(name="ring", bufs=3))
         psum = ctx.enter_context(tc.psum_pool(name="psum", bufs=8))
 
         offsets = keep.tile([P, T // 16], U16, name="offsets")
 
-        def load(rows, shape):
-            raw = raws.tile(shape, F32, name="raw", tag="raw")
+        def load(rows, shape, tag):
+            raw = raws.tile(shape, F32, name="raw", tag=tag, align_bytes=64)
             nc.sync.dma_start(out=raw[:], in_=rows)
             return raw
 
@@ -70,11 +73,11 @@ def tile_moe_prv_lin_relu2_kernel(tc, uT, wu, w, b, gate, offs, out):
 
         def load_wu(g):
             rows = wu[g * K_PASS : (g + 1) * K_PASS, :].rearrange("(p j) c -> p j c", j=PACK)
-            wu_raw[g] = load(rows, [P, PACK, K])
+            wu_raw[g] = load(rows, [P, PACK, K], "wu%d" % g)
 
         def load_u(g, t0, width):
             rows = uT[g * K_PASS : (g + 1) * K_PASS, t0 : t0 + width].rearrange("(p j) t -> p j t", j=PACK)
-            u_raw[g, t0] = load(rows, [P, PACK, width])
+            u_raw[g, t0] = load(rows, [P, PACK, width], "u%d_%d" % (g, t0))
 
         for t0, width in TOKEN_LOADS:
             for g in range(PASSES):
@@ -82,16 +85,17 @@ def tile_moe_prv_lin_relu2_kernel(tc, uT, wu, w, b, gate, offs, out):
                     load_wu(g)
                 load_u(g, t0, width)
         nc.sync.dma_start(offsets[:], offs)
-        bias = keep.tile([P, 2, E], F32, name="bias")
-        nc.sync.dma_start(out=bias[:], in_=b.rearrange("(h p) e -> p h e", p=P))
-        gates = keep.tile([P, 2, T], F32, name="gates")
+        bias = keep.tile([P, 2, 16], F32, name="bias")
+        gates = [keep.tile([P, 2, GATE_LOAD], F32, name="gates%d" % i) for i in range(T // GATE_LOAD)]
         w_raw = []
         for q in range(E // 2):
             rows = w[2 * q : 2 * q + 2].rearrange("e (p j) n -> p e (j n)", j=PACK)
-            w_raw.append(load(rows, [P, 2, PACK * N]))
+            w_raw.append(load(rows, [P, 2, PACK * N], W_SLOTS[q]))
+            if q == 1:
+                nc.sync.dma_start(out=bias[:, :, :E], in_=b.rearrange("(h p) e -> p h e", p=P))
             if 2 <= q < 2 + T // GATE_LOAD:
                 cols = slice((q - 2) * GATE_LOAD, (q - 1) * GATE_LOAD)
-                nc.sync.dma_start(out=gates[:, :, cols], in_=gate[:, cols].rearrange("(h p) s -> p h s", p=P))
+                nc.sync.dma_start(out=gates[q - 2][:], in_=gate[:, cols].rearrange("(h p) s -> p h s", p=P))
 
         wu_mx = [mx_tiles("wu%d" % g, K) for g in range(PASSES)]
         u_mx = [mx_tiles("u%d" % g, T) for g in range(PASSES)]
@@ -111,9 +115,9 @@ def tile_moe_prv_lin_relu2_kernel(tc, uT, wu, w, b, gate, offs, out):
             interleave(copy, grouped[:], u_raw[g, start][:, :, t0 - start : t0 - start + n])
             return u_mx[g], slice(t0, t0 + n), grouped[:]
 
-        def project(t0, n, copies):
+        def project(t0, n, copies, which=(0, 1)):
             cols = slice(t0, t0 + n)
-            for a in range(2):
+            for a in which:
                 acc = psum.tile([P, 2, n], F32, name="acc", tag="acc")
                 for e in range(2):
                     j = 2 * a + e
@@ -145,13 +149,15 @@ def tile_moe_prv_lin_relu2_kernel(tc, uT, wu, w, b, gate, offs, out):
         u03 = cast_u(on_v, 0, 1280, 256)
         quantize(*u12)
         project(1024, 256, (on_s, on_s))
-        u13a = cast_u(on_v, 1, 1280, 128)
         quantize(*u03)
+        u13a = cast_u(on_v, 1, 1280, 128)
         u13b = cast_u(on_v, 1, 1408, 128)
         quantize(*u13a)
         quantize(*u13b)
-        project(1280, 128, (on_s, on_s))
-        project(1408, 128, (on_v, on_s))
+        project(1280, 128, (on_s, on_s), (0,))
+        project(1408, 128, (on_v, on_s), (0,))
+        project(1280, 128, (on_s, on_s), (1,))
+        project(1408, 128, (on_v, on_s), (1,))
 
         x_mx = mx_tiles("x", T)
         w_mx = mx_tiles("w", E * N)
@@ -163,7 +169,7 @@ def tile_moe_prv_lin_relu2_kernel(tc, uT, wu, w, b, gate, offs, out):
 
         def gather(i):
             s0, n = GATHERS[i]
-            tag = "slots%d" % (i - 2) if i >= 2 else "picked%d" % i
+            tag = "picked%d" % i
             picked[i] = keep.tile([P, 2, 2 * n], BF16, name="picked", tag=tag, align_bytes=64)
             for a in range(2):
                 nc.vector.tensor_copy(
@@ -173,7 +179,10 @@ def tile_moe_prv_lin_relu2_kernel(tc, uT, wu, w, b, gate, offs, out):
 
         def prepare_x(i):
             s0, n = GATHERS[i]
-            grouped = keep.tile([P, n * PACK], BF16, name="x_grouped", tag="slots%d" % i, align_bytes=64)
+            if i == 2:
+                grouped = raws.tile([P, n * PACK], BF16, name="x_grouped", tag=W_SLOTS[2], align_bytes=64)
+            else:
+                grouped = keep.tile([P, n * PACK], BF16, name="x_grouped", tag="slots%d" % i, align_bytes=64)
             nc.scalar.copy(
                 out=grouped[:].bitcast(F32).rearrange("p (s a) -> p s a", a=2),
                 in_=picked[i][:].bitcast(F32).rearrange("p a s -> p s a"),
@@ -181,54 +190,64 @@ def tile_moe_prv_lin_relu2_kernel(tc, uT, wu, w, b, gate, offs, out):
             quantize(x_mx, slice(s0, s0 + n), grouped[:])
 
         def prepare_w(q):
-            grouped = ring.tile([P, 2 * N * PACK], BF16, name="w_grouped", tag="w_grouped", align_bytes=64)
-            nc.scalar.copy(
-                out=grouped[:].rearrange("p (e c i j) -> p e c j i", e=2, i=4, j=PACK),
-                in_=w_raw[q][:].rearrange("p e (j c i) -> p e c j i", j=PACK, i=4),
-            )
+            if q < 3:
+                grouped = ring.tile([P, 2 * N * PACK], BF16, name="w_grouped", tag="w_grouped", align_bytes=64)
+            else:
+                grouped = raws.tile([P, 2 * N * PACK], BF16, name="w_grouped", tag=W_SLOTS[RELU_SLOTS[q - 2]], align_bytes=64)
+            if q < 2:
+                for e in range(2):
+                    nc.gpsimd.tensor_scalar(
+                        out=grouped[:, e * N * PACK : (e + 1) * N * PACK].rearrange("p (n j) -> p n j", j=PACK),
+                        in0=w_raw[q][:, e, :].rearrange("p (j n) -> p n j", j=PACK),
+                        scalar1=1.0,
+                        scalar2=0.0,
+                        op0=MULT,
+                        op1=ADD,
+                    )
+            else:
+                nc.scalar.copy(
+                    out=grouped[:].rearrange("p (e c i j) -> p e c j i", e=2, i=4, j=PACK),
+                    in_=w_raw[q][:].rearrange("p e (j c i) -> p e c j i", j=PACK, i=4),
+                )
             quantize(w_mx, slice(2 * q * N, 2 * (q + 1) * N), grouped[:])
 
-        def experts(e0, count, h):
-            width = count * C
-            acc = psum.tile([P, width], F32, name="acc", tag="acc")
-            relu = ring.tile([P, width], F32, name="relu", tag="relu%d" % count, bufs=3 if count == 2 else 1)
-            for i in range(count):
-                e = e0 + i
-                matmul(acc[:, i * C : (i + 1) * C], w_mx, slice(e * N + h * P, e * N + (h + 1) * P),
-                       x_mx, slice(e * C, (e + 1) * C), True, True)
-            for i in range(count):
-                nc.scalar.activation(out=relu[:, i * C : (i + 1) * C], in_=acc[:, i * C : (i + 1) * C],
-                                     func=ACT.Relu, bias=bias[:, h, e0 + i : e0 + i + 1])
-            squared = ring.tile([P, width], F32, name="squared", tag="squared", bufs=6)
-            nc.scalar.activation(out=squared[:], in_=relu[:], func=ACT.Square)
-            nc.vector.tensor_tensor(
-                windows[h][:].indirect(slot_offsets(e0 * C, width)),
-                squared[:],
-                gates[:, h, e0 * C : e0 * C + width],
-                MULT,
-            )
-            if e0 + count == E:
-                nc.sync.dma_start(out=out[h * P : (h + 1) * P, :], in_=windows[h][:])
+        def experts(q):
+            tag = W_SLOTS[RELU_SLOTS[q]]
+            relu = raws.tile([P, 2, PAIR], F32, name="relu", tag=tag, align_bytes=64)
+            for h in range(2):
+                acc = psum.tile([P, PAIR], F32, name="acc", tag="acc")
+                for i in range(2):
+                    e = 2 * q + i
+                    matmul(acc[:, i * C : (i + 1) * C], w_mx, slice(e * N + h * P, e * N + (h + 1) * P),
+                           x_mx, slice(e * C, (e + 1) * C), True, True)
+                for i in range(2):
+                    e = 2 * q + i
+                    nc.scalar.activation(out=relu[:, h, i * C : (i + 1) * C], in_=acc[:, i * C : (i + 1) * C],
+                                         func=ACT.Relu, bias=bias[:, h, e : e + 1])
+            g0 = q * PAIR % GATE_LOAD
+            for h in range(2):
+                squared = ring.tile([P, PAIR], F32, name="squared", tag="squared", bufs=6)
+                nc.scalar.activation(out=squared[:], in_=relu[:, h, :], func=ACT.Square)
+                nc.vector.tensor_tensor(
+                    windows[h][:].indirect(slot_offsets(q * PAIR, PAIR)),
+                    squared[:],
+                    gates[q * PAIR // GATE_LOAD][:, h, g0 : g0 + PAIR],
+                    MULT,
+                )
+                if q == E // 2 - 1:
+                    nc.sync.dma_start(out=out[h * P : (h + 1) * P, :], in_=windows[h][:])
 
-        gather(0)
-        gather(1)
+        for i in range(3):
+            gather(i)
         prepare_w(0)
         prepare_x(0)
-        gather(2)
         prepare_w(1)
-        prepare_x(1)
-        experts(0, 2, 0)
-        experts(0, 2, 1)
-        prepare_x(2)
-        experts(2, 2, 0)
         prepare_w(2)
-        experts(2, 2, 1)
-        experts(4, 2, 0)
-        prepare_w(3)
-        experts(4, 2, 1)
-        experts(6, 2, 0)
-        prepare_w(4)
-        prepare_w(5)
-        experts(6, 2, 1)
-        experts(8, 4, 0)
-        experts(8, 4, 1)
+        prepare_x(1)
+        experts(0)
+        prepare_x(2)
+        experts(1)
+        for q in range(2, E // 2):
+            if q + 1 < E // 2:
+                prepare_w(q + 1)
+            experts(q)

@@ -24,8 +24,9 @@ TOKEN_LOADS = ((0, 512), (512, 512), (1024, 256), (1280, 256))
 GATHERS = ((0, 512), (512, 512), (1024, 512))
 GATE_LOAD = 512
 PAIR = 2 * C
-RELU_SLOTS = (2, 1, 3, 4, 5, 0)
-W_SLOTS = ("w0", "wu0", "u0_0", "wu1", "u1_0", "u0_512")
+GATES_AFTER = {3: (0,), 5: (1, 2)}
+GPSIMD_EXPERTS = (1, 2, 3, 4)
+W_SLOTS = (("w0",), ("wu0", "u1_512"), ("u1_1280", "u0_0"), ("wu1", "u0_1024"), ("u1_0", "u1_1024"), ("u0_512", "u0_1280"))
 
 
 def tile_moe_prv_lin_relu2_kernel(tc, uT, wu, w, b, gate, offs, out):
@@ -89,13 +90,19 @@ def tile_moe_prv_lin_relu2_kernel(tc, uT, wu, w, b, gate, offs, out):
         gates = [keep.tile([P, 2, GATE_LOAD], F32, name="gates%d" % i) for i in range(T // GATE_LOAD)]
         w_raw = []
         for q in range(E // 2):
-            rows = w[2 * q : 2 * q + 2].rearrange("e (p j) n -> p e (j n)", j=PACK)
-            w_raw.append(load(rows, [P, 2, PACK * N], W_SLOTS[q]))
-            if q == 1:
+            if len(W_SLOTS[q]) == 1:
+                rows = w[2 * q : 2 * q + 2].rearrange("e (p j) n -> p e j n", j=PACK)
+                both = load(rows, [P, 2, PACK, N], W_SLOTS[q][0])
+                w_raw.extend([both[:, 0], both[:, 1]])
+            else:
+                for i in range(2):
+                    rows = w[2 * q + i].rearrange("(p j) n -> p j n", j=PACK)
+                    w_raw.append(load(rows, [P, PACK, N], W_SLOTS[q][i])[:])
+            if q == 2:
                 nc.sync.dma_start(out=bias[:, :, :E], in_=b.rearrange("(h p) e -> p h e", p=P))
-            if 2 <= q < 2 + T // GATE_LOAD:
-                cols = slice((q - 2) * GATE_LOAD, (q - 1) * GATE_LOAD)
-                nc.sync.dma_start(out=gates[q - 2][:], in_=gate[:, cols].rearrange("(h p) s -> p h s", p=P))
+            for i in GATES_AFTER.get(q, ()):
+                cols = slice(i * GATE_LOAD, (i + 1) * GATE_LOAD)
+                nc.sync.dma_start(out=gates[i][:], in_=gate[:, cols].rearrange("(h p) s -> p h s", p=P))
 
         wu_mx = [mx_tiles("wu%d" % g, K) for g in range(PASSES)]
         u_mx = [mx_tiles("u%d" % g, T) for g in range(PASSES)]
@@ -129,9 +136,9 @@ def tile_moe_prv_lin_relu2_kernel(tc, uT, wu, w, b, gate, offs, out):
                 )
 
         on_s, on_v = nc.scalar.copy, nc.vector.tensor_copy
-        wu0 = cast_wu(on_s, 0)
-        u00 = cast_u(on_v, 0, 0, 512)
+        wu0 = cast_wu(on_v, 0)
         quantize(*wu0)
+        u00 = cast_u(on_v, 0, 0, 512)
         quantize(*u00)
         quantize(*cast_wu(on_v, 1))
         u10a = cast_u(on_s, 1, 0, 256)
@@ -163,6 +170,7 @@ def tile_moe_prv_lin_relu2_kernel(tc, uT, wu, w, b, gate, offs, out):
         w_mx = mx_tiles("w", E * N)
         windows = [keep.tile([P, T], F32, name="window%d" % h) for h in range(2)]
         picked = {}
+        shared = []
 
         def slot_offsets(s0, n):
             return offsets[:, s0 // 16 : (s0 + n) // 16]
@@ -180,41 +188,46 @@ def tile_moe_prv_lin_relu2_kernel(tc, uT, wu, w, b, gate, offs, out):
         def prepare_x(i):
             s0, n = GATHERS[i]
             if i == 2:
-                grouped = raws.tile([P, n * PACK], BF16, name="x_grouped", tag=W_SLOTS[2], align_bytes=64)
+                grouped = shared[0][:, 4 * PAIR :].bitcast(BF16)
             else:
-                grouped = keep.tile([P, n * PACK], BF16, name="x_grouped", tag="slots%d" % i, align_bytes=64)
+                grouped = keep.tile([P, n * PACK], BF16, name="x_grouped%d" % i, align_bytes=64)[:]
             nc.scalar.copy(
-                out=grouped[:].bitcast(F32).rearrange("p (s a) -> p s a", a=2),
+                out=grouped.bitcast(F32).rearrange("p (s a) -> p s a", a=2),
                 in_=picked[i][:].bitcast(F32).rearrange("p a s -> p s a"),
             )
-            quantize(x_mx, slice(s0, s0 + n), grouped[:])
+            quantize(x_mx, slice(s0, s0 + n), grouped)
 
         def prepare_w(q):
             if q < 3:
                 grouped = ring.tile([P, 2 * N * PACK], BF16, name="w_grouped", tag="w_grouped", align_bytes=64)
             else:
-                grouped = raws.tile([P, 2 * N * PACK], BF16, name="w_grouped", tag=W_SLOTS[RELU_SLOTS[q - 2]], align_bytes=64)
-            if q < 2:
-                for e in range(2):
+                grouped = raws.tile([P, 2 * N * PACK], BF16, name="w_grouped", tag=W_SLOTS[q - 1][1 if q == 3 else 0], align_bytes=64)
+            for i in range(2):
+                e = 2 * q + i
+                words = grouped[:, i * N * PACK : (i + 1) * N * PACK]
+                if e in GPSIMD_EXPERTS:
                     nc.gpsimd.tensor_scalar(
-                        out=grouped[:, e * N * PACK : (e + 1) * N * PACK].rearrange("p (n j) -> p n j", j=PACK),
-                        in0=w_raw[q][:, e, :].rearrange("p (j n) -> p n j", j=PACK),
+                        out=words.rearrange("p (n j) -> p n j", j=PACK),
+                        in0=w_raw[e].rearrange("p j n -> p n j"),
                         scalar1=1.0,
                         scalar2=0.0,
                         op0=MULT,
                         op1=ADD,
                     )
-            else:
-                nc.scalar.copy(
-                    out=grouped[:].rearrange("p (e c i j) -> p e c j i", e=2, i=4, j=PACK),
-                    in_=w_raw[q][:].rearrange("p e (j c i) -> p e c j i", j=PACK, i=4),
-                )
+                else:
+                    interleave(nc.scalar.copy, words, w_raw[e])
             quantize(w_mx, slice(2 * q * N, 2 * (q + 1) * N), grouped[:])
+            if q == 2:
+                shared.append(raws.tile([P, 8 * PAIR], F32, name="shared", tag=W_SLOTS[2][1], align_bytes=64))
 
         def experts(q):
-            tag = W_SLOTS[RELU_SLOTS[q]]
-            relu = raws.tile([P, 2, PAIR], F32, name="relu", tag=tag, align_bytes=64)
+            relu = []
             for h in range(2):
+                if q < 2:
+                    relu.append(shared[0][:, (2 * q + h) * PAIR : (2 * q + h + 1) * PAIR])
+                else:
+                    tag = W_SLOTS[q + 1][h] if q + 1 < len(W_SLOTS) else W_SLOTS[h][0]
+                    relu.append(raws.tile([P, PAIR], F32, name="relu", tag=tag, align_bytes=64)[:])
                 acc = psum.tile([P, PAIR], F32, name="acc", tag="acc")
                 for i in range(2):
                     e = 2 * q + i
@@ -222,12 +235,12 @@ def tile_moe_prv_lin_relu2_kernel(tc, uT, wu, w, b, gate, offs, out):
                            x_mx, slice(e * C, (e + 1) * C), True, True)
                 for i in range(2):
                     e = 2 * q + i
-                    nc.scalar.activation(out=relu[:, h, i * C : (i + 1) * C], in_=acc[:, i * C : (i + 1) * C],
+                    nc.scalar.activation(out=relu[h][:, i * C : (i + 1) * C], in_=acc[:, i * C : (i + 1) * C],
                                          func=ACT.Relu, bias=bias[:, h, e : e + 1])
             g0 = q * PAIR % GATE_LOAD
             for h in range(2):
                 squared = ring.tile([P, PAIR], F32, name="squared", tag="squared", bufs=6)
-                nc.scalar.activation(out=squared[:], in_=relu[:, h, :], func=ACT.Square)
+                nc.scalar.activation(out=squared[:], in_=relu[h], func=ACT.Square)
                 nc.vector.tensor_tensor(
                     windows[h][:].indirect(slot_offsets(q * PAIR, PAIR)),
                     squared[:],
@@ -242,10 +255,10 @@ def tile_moe_prv_lin_relu2_kernel(tc, uT, wu, w, b, gate, offs, out):
         prepare_w(0)
         prepare_x(0)
         prepare_w(1)
-        prepare_w(2)
         prepare_x(1)
-        experts(0)
+        prepare_w(2)
         prepare_x(2)
+        experts(0)
         experts(1)
         for q in range(2, E // 2):
             if q + 1 < E // 2:

from contextlib import ExitStack

import concourse.mybir as mybir

K, T, E, C, N, M = 512, 1536, 12, 128, 256, 1024
FLOPS = 2 * M * K * T + 2 * K * N * E * C

F32 = mybir.dt.float32
BF16 = mybir.dt.bfloat16
U32 = mybir.dt.uint32
U16 = mybir.dt.uint16
U8 = mybir.dt.uint8
FP8X4 = mybir.dt.float8_e4m3fn_x4
ACT = mybir.ActivationFunctionType
MULT = mybir.AluOpType.mult
ADD = mybir.AluOpType.add

P = 128
PACK = 4
K_PASS = P * PACK
PASSES = M // K_PASS
SUB = 256
TOKEN_LOADS = ((0, 512), (512, 512), (1024, 256), (1280, 256))
GATHERS = ((0, 512), (512, 512), (1024, 512))
GATE_LOAD = 512
PAIR = 2 * C
GATES_AFTER = {3: (0,), 5: (1, 2)}
GPSIMD_EXPERTS = (1, 2, 3, 4)
W_SLOTS = (("w0",), ("wu0", "u1_512"), ("u1_1280", "u0_0"), ("wu1", "u0_1024"), ("u1_0", "u1_1024"), ("u0_512", "u0_1280"))


def tile_moe_prv_lin_relu2_kernel(tc, uT, wu, w, b, gate, offs, out):
    nc = tc.nc

    with ExitStack() as ctx:
        keep = ctx.enter_context(tc.tile_pool(name="keep", bufs=1))
        raws = ctx.enter_context(tc.tile_pool(name="raws", bufs=1))
        ring = ctx.enter_context(tc.tile_pool(name="ring", bufs=3))
        psum = ctx.enter_context(tc.psum_pool(name="psum", bufs=8))

        offsets = keep.tile([P, T // 16], U16, name="offsets")

        def load(rows, shape, tag):
            raw = raws.tile(shape, F32, name="raw", tag=tag, align_bytes=64)
            nc.sync.dma_start(out=raw[:], in_=rows)
            return raw

        def mx_tiles(name, width):
            codes = keep.tile([P, width], U32, name=name + "_codes", align_bytes=64)
            scales = keep.tile([P, width], U8, name=name + "_scales", align_bytes=64)
            return codes, scales

        def quantize(mx, cols, grouped):
            nc.vector.quantize_mx(out=mx[0][:, cols].bitcast(FP8X4), scales=mx[1][:, cols], in_=grouped)

        def interleave(copy, grouped, rows):
            copy(
                out=grouped.rearrange("p (c i j) -> p c j i", i=4, j=PACK),
                in_=rows.rearrange("p j (c i) -> p c j i", i=4),
            )

        def matmul(acc, lhs, lhs_cols, rhs, rhs_cols, start, stop):
            nc.tensor.matmul_mx(
                out=acc,
                lhsT=lhs[0][:, lhs_cols].bitcast(FP8X4),
                lhsT_scale=lhs[1][:, lhs_cols],
                rhs=rhs[0][:, rhs_cols].bitcast(FP8X4),
                rhs_scale=rhs[1][:, rhs_cols],
                start=start,
                stop=stop,
            )

        wu_raw, u_raw = {}, {}

        def load_wu(g):
            rows = wu[g * K_PASS : (g + 1) * K_PASS, :].rearrange("(p j) c -> p j c", j=PACK)
            wu_raw[g] = load(rows, [P, PACK, K], "wu%d" % g)

        def load_u(g, t0, width):
            rows = uT[g * K_PASS : (g + 1) * K_PASS, t0 : t0 + width].rearrange("(p j) t -> p j t", j=PACK)
            u_raw[g, t0] = load(rows, [P, PACK, width], "u%d_%d" % (g, t0))

        for t0, width in TOKEN_LOADS:
            for g in range(PASSES):
                if t0 == 0:
                    load_wu(g)
                load_u(g, t0, width)
        nc.sync.dma_start(offsets[:], offs)
        bias = keep.tile([P, 2, 16], F32, name="bias")
        gates = [keep.tile([P, 2, GATE_LOAD], F32, name="gates%d" % i) for i in range(T // GATE_LOAD)]
        w_raw = []
        for q in range(E // 2):
            if len(W_SLOTS[q]) == 1:
                rows = w[2 * q : 2 * q + 2].rearrange("e (p j) n -> p e j n", j=PACK)
                both = load(rows, [P, 2, PACK, N], W_SLOTS[q][0])
                w_raw.extend([both[:, 0], both[:, 1]])
            else:
                for i in range(2):
                    rows = w[2 * q + i].rearrange("(p j) n -> p j n", j=PACK)
                    w_raw.append(load(rows, [P, PACK, N], W_SLOTS[q][i])[:])
            if q == 2:
                nc.sync.dma_start(out=bias[:, :, :E], in_=b.rearrange("(h p) e -> p h e", p=P))
            for i in GATES_AFTER.get(q, ()):
                cols = slice(i * GATE_LOAD, (i + 1) * GATE_LOAD)
                nc.sync.dma_start(out=gates[i][:], in_=gate[:, cols].rearrange("(h p) s -> p h s", p=P))

        wu_mx = [mx_tiles("wu%d" % g, K) for g in range(PASSES)]
        u_mx = [mx_tiles("u%d" % g, T) for g in range(PASSES)]
        x_pairs = [keep.tile([P, 2 * T], BF16, name="x_pairs%d" % a) for a in range(2)]

        def cast_wu(copy, g):
            grouped = ring.tile([P, K * PACK], BF16, name="wu_grouped", tag="w_grouped", align_bytes=64)
            copy(
                out=grouped[:].rearrange("p (t m j) -> p m t j", t=PACK, j=PACK),
                in_=wu_raw[g][:].rearrange("p j (m t) -> p m t j", t=PACK),
            )
            return wu_mx[g], slice(0, K), grouped[:]

        def cast_u(copy, g, t0, n):
            start = max(s for s, width in TOKEN_LOADS if s <= t0)
            grouped = ring.tile([P, n * PACK], BF16, name="u_grouped", tag="u_grouped", bufs=4, align_bytes=64)
            interleave(copy, grouped[:], u_raw[g, start][:, :, t0 - start : t0 - start + n])
            return u_mx[g], slice(t0, t0 + n), grouped[:]

        def project(t0, n, copies, which=(0, 1)):
            cols = slice(t0, t0 + n)
            for a in which:
                acc = psum.tile([P, 2, n], F32, name="acc", tag="acc")
                for e in range(2):
                    j = 2 * a + e
                    for g in range(PASSES):
                        matmul(acc[:, e, :], wu_mx[g], slice(j * P, (j + 1) * P), u_mx[g], cols, g == 0, g == PASSES - 1)
                copies[a](
                    out=x_pairs[a][:, 2 * t0 : 2 * (t0 + n)].rearrange("p (n e) -> p n e", e=2),
                    in_=acc[:].rearrange("p e n -> p n e"),
                )

        on_s, on_v = nc.scalar.copy, nc.vector.tensor_copy
        wu0 = cast_wu(on_v, 0)
        quantize(*wu0)
        u00 = cast_u(on_v, 0, 0, 512)
        quantize(*u00)
        quantize(*cast_wu(on_v, 1))
        u10a = cast_u(on_s, 1, 0, 256)
        quantize(*cast_u(on_v, 1, 256, 256))
        quantize(*u10a)
        project(256, 256, (on_s, on_s))
        project(0, 256, (on_s, on_s))
        quantize(*cast_u(on_v, 0, 512, 512))
        quantize(*cast_u(on_v, 1, 512, 512))
        u02 = cast_u(on_s, 0, 1024, 256)
        project(512, 256, (on_s, on_s))
        project(768, 256, (on_s, on_s))
        u12 = cast_u(on_v, 1, 1024, 256)
        quantize(*u02)
        u03 = cast_u(on_v, 0, 1280, 256)
        quantize(*u12)
        project(1024, 256, (on_s, on_s))
        quantize(*u03)
        u13a = cast_u(on_v, 1, 1280, 128)
        u13b = cast_u(on_v, 1, 1408, 128)
        quantize(*u13a)
        quantize(*u13b)
        project(1280, 128, (on_s, on_s), (0,))
        project(1408, 128, (on_v, on_s), (0,))
        project(1280, 128, (on_s, on_s), (1,))
        project(1408, 128, (on_v, on_s), (1,))

        x_mx = mx_tiles("x", T)
        w_mx = mx_tiles("w", E * N)
        windows = [keep.tile([P, T], F32, name="window%d" % h) for h in range(2)]
        picked = {}
        shared = []

        def slot_offsets(s0, n):
            return offsets[:, s0 // 16 : (s0 + n) // 16]

        def gather(i):
            s0, n = GATHERS[i]
            tag = "picked%d" % i
            picked[i] = keep.tile([P, 2, 2 * n], BF16, name="picked", tag=tag, align_bytes=64)
            for a in range(2):
                nc.vector.tensor_copy(
                    out=picked[i][:, a, :].bitcast(U32),
                    in_=x_pairs[a][:].bitcast(U32).indirect(slot_offsets(s0, n)),
                )

        def prepare_x(i):
            s0, n = GATHERS[i]
            if i == 2:
                grouped = shared[0][:, 4 * PAIR :].bitcast(BF16)
            else:
                grouped = keep.tile([P, n * PACK], BF16, name="x_grouped%d" % i, align_bytes=64)[:]
            nc.scalar.copy(
                out=grouped.bitcast(F32).rearrange("p (s a) -> p s a", a=2),
                in_=picked[i][:].bitcast(F32).rearrange("p a s -> p s a"),
            )
            quantize(x_mx, slice(s0, s0 + n), grouped)

        def prepare_w(q):
            if q < 3:
                grouped = ring.tile([P, 2 * N * PACK], BF16, name="w_grouped", tag="w_grouped", align_bytes=64)
            else:
                grouped = raws.tile([P, 2 * N * PACK], BF16, name="w_grouped", tag=W_SLOTS[q - 1][1 if q == 3 else 0], align_bytes=64)
            for i in range(2):
                e = 2 * q + i
                words = grouped[:, i * N * PACK : (i + 1) * N * PACK]
                if e in GPSIMD_EXPERTS:
                    nc.gpsimd.tensor_scalar(
                        out=words.rearrange("p (n j) -> p n j", j=PACK),
                        in0=w_raw[e].rearrange("p j n -> p n j"),
                        scalar1=1.0,
                        scalar2=0.0,
                        op0=MULT,
                        op1=ADD,
                    )
                else:
                    interleave(nc.scalar.copy, words, w_raw[e])
            quantize(w_mx, slice(2 * q * N, 2 * (q + 1) * N), grouped[:])
            if q == 2:
                shared.append(raws.tile([P, 8 * PAIR], F32, name="shared", tag=W_SLOTS[2][1], align_bytes=64))

        def experts(q):
            relu = []
            for h in range(2):
                if q < 2:
                    relu.append(shared[0][:, (2 * q + h) * PAIR : (2 * q + h + 1) * PAIR])
                else:
                    tag = W_SLOTS[q + 1][h] if q + 1 < len(W_SLOTS) else W_SLOTS[h][0]
                    relu.append(raws.tile([P, PAIR], F32, name="relu", tag=tag, align_bytes=64)[:])
                acc = psum.tile([P, PAIR], F32, name="acc", tag="acc")
                for i in range(2):
                    e = 2 * q + i
                    matmul(acc[:, i * C : (i + 1) * C], w_mx, slice(e * N + h * P, e * N + (h + 1) * P),
                           x_mx, slice(e * C, (e + 1) * C), True, True)
                for i in range(2):
                    e = 2 * q + i
                    nc.scalar.activation(out=relu[h][:, i * C : (i + 1) * C], in_=acc[:, i * C : (i + 1) * C],
                                         func=ACT.Relu, bias=bias[:, h, e : e + 1])
            g0 = q * PAIR % GATE_LOAD
            for h in range(2):
                squared = ring.tile([P, PAIR], F32, name="squared", tag="squared", bufs=6)
                nc.scalar.activation(out=squared[:], in_=relu[h], func=ACT.Square)
                nc.vector.tensor_tensor(
                    windows[h][:].indirect(slot_offsets(q * PAIR, PAIR)),
                    squared[:],
                    gates[q * PAIR // GATE_LOAD][:, h, g0 : g0 + PAIR],
                    MULT,
                )
                if q == E // 2 - 1:
                    nc.sync.dma_start(out=out[h * P : (h + 1) * P, :], in_=windows[h][:])

        for i in range(3):
            gather(i)
        prepare_w(0)
        prepare_x(0)
        prepare_w(1)
        prepare_x(1)
        prepare_w(2)
        prepare_x(2)
        experts(0)
        experts(1)
        for q in range(2, E // 2):
            if q + 1 < E // 2:
                prepare_w(q + 1)
            experts(q)
